import numpy as np, ml_dtypes
CORES = [65,73,81,89,97,105,113,121]
N = 8
import mx_ref
NC, WT = 512, 1
BF = ml_dtypes.bfloat16
def pk(c, s, i=0):
    return (np.ascontiguousarray(c[:, 512 * i:512 * i + 512]), mx_ref.live(s[:, 128 * i:128 * i + 128]))
def inputs(rng, e, E):
    def f(*shape):
        v = (rng.standard_normal(shape, dtype=np.float32) * np.exp2(rng.integers(-2, 3, shape[:-1] + (1,)))).astype(BF)
        return mx_ref.spread((v.astype(np.float32) * np.exp2(rng.integers(-E, E + 1, shape[:-2] + (1, 1))).astype(np.float32)).astype(BF), rng, e)
    def packed(k):
        c = np.zeros((N, 128, k * 512), np.uint8); s = np.zeros((N, 128, k * 128), np.uint8)
        for r in range(N):
            for i in range(k):
                a, b = mx_ref.quantize(f(128, 512)); c[r][:, 512 * i:512 * i + 512] = a; s[r][:, 128 * i:128 * i + 128] = mx_ref.plane(b, rng)
        return c, s
    d = {}
    d["wc"], d["ws"] = packed(WT)
    d["x"] = f(N, 128, 4 * NC)
    return d
def setup_inputs(rng):
    return inputs(rng, 0, 0)
def setup_inputs_blocks(rng):
    return inputs(rng, 4, 0)
def setup_inputs_wide(rng):
    return inputs(rng, 0, 8)
def reference(wc, ws, x):
    y = np.zeros((N, 128, N * WT * NC), np.float32)
    for r in range(N):
        X = mx_ref.quantize(x[r])
        for b in range(N * WT):
            y[r][:, NC * b:NC * b + NC] = mx_ref.matmul(pk(wc[b // WT], ws[b // WT], b % WT), X)
    return {"y": y}

from concourse.bass import DstId, RemoteDMATransfer
from concourse.mybir import dt, ActivationFunctionType

N = 8
NC = 512
WW = 128

SCRATCH = {
    "wcd": ("dram", [128, WW], "float8_e4m3fn_x4"),
    "wsd": ("dram", [128, WW], "uint8"),
    "wq": ("sbuf", [128, WW * N], "float8_e4m3fn_x4"),
    "wp": ("sbuf", [128, WW * N], "uint8"),
    "xt": ("sbuf", [128, 4 * NC], "bfloat16"),
    "xq": ("sbuf", [128, NC], "float8_e4m3fn_x4"),
    "xp": ("sbuf", [128, NC], "uint8"),
    "ps": ("psum", [128, NC * N], "float32"),
    "yo": ("sbuf", [128, NC * N], "float32"),
}
SEMAPHORES = (["ls", "lc", "lw", "lx", "qx", "hs", "hc", "sent", "st"]
              + ["a%d" % j for j in range(N)] + ["m%d" % j for j in range(N)] + ["c%d" % j for j in range(N)])


def _engines(mask):
    return bin(mask).count("1")


def _routes(T, topo, r):
    cores = T.cores
    me = cores[r]
    chips = [topo.chip(c) for c in cores]

    def mate_of(i):
        return [j for j in range(len(cores)) if topo.mates(chips[i], chips[j])][0]

    ring = [j for j in range(len(cores)) if j == r or topo.same_plane(chips[r], chips[j])]
    k = ring.index(r)
    near = [ring[(k + o) % len(ring)] for o in range(1, len(ring))]
    far = [mate_of(j) for j in near]
    spare = [c for c in range(topo.CHIPS * topo.CORES_PER_CHIP) if topo.chip(c) == chips[r] and T.rank_of(c) is None]
    port = [c for c in spare if topo.may_write(c, cores[mate_of(r)])]
    plain = [c for c in spare if c not in port]
    here = [c for c in spare if topo.die(c) == topo.die(me)]
    p1, p0 = [c for c in port if c in here], [c for c in port if c not in here]
    q1, q0 = [c for c in plain if c in here], [c for c in plain if c not in here]
    jobs = [(p1[0], mate_of(r)), (p1[1], far[0]), (q1[0], near[1]), (p0[0], far[1]), (q0[0], near[2]), (p0[1], far[2])]
    return near[0], jobs


def _send(g, T, topo, src, dst_rank, slot):
    dst = T.cores[dst_rank]
    rid, pid, _ = topo.addr(dst)
    mask = topo.mask(src, dst)
    cols = slice(WW * slot, WW * slot + WW)
    return rid, pid, mask, cols


def rank_program(g, core, T, topo):
    rank = T.rank_of(core)
    S = T.sem

    if rank is None:
        owners = [r for r in range(N) if topo.chip(T.cores[r]) == topo.chip(core)]
        if not owners:
            return
        r = owners[0]
        mine = [d for (h, d) in _routes(T, topo, r)[1] if h == core]
        if not mine:
            return
        fan = _engines(topo.mask(T.cores[r], core) & ~topo.mask(T.cores[r], T.cores[mine[0]]))
        rid, pid, mask, cols = _send(g, T, topo, core, mine[0], r)
        g.wait_ge(S.hs, fan)
        g.remote_dma(T.wp[:, cols], T.wsd[:], S["a%d" % r], S.sent, pid, rid, mask)
        g.wait_ge(S.hc, fan)
        g.remote_dma(T.wq[:, cols].bitcast(dt.uint8), T.wcd[:].bitcast(dt.uint8), S["a%d" % r], S.sent, pid, rid, mask)
        g.wait_ge(S.sent, 2 * _engines(mask))
        return

    direct, jobs = _routes(T, topo, rank)
    own = slice(WW * rank, WW * rank + WW)

    g.sync.dma_start(T.wsd[:], T.ws[:]).then_inc(S.ls, 16)
    g.scalar.dma_start(T.wcd[:].bitcast(dt.uint8), T.wc[:]).then_inc(S.lc, 16)
    g.sync.dma_start(T.xt[:], T.x[:]).then_inc(S.lx, 16)
    g.scalar.dma_start(T.wq[:, own].bitcast(dt.uint8), T.wc[:]).then_inc(S.lw, 16)
    g.scalar.dma_start(T.wp[:, own], T.ws[:]).then_inc(S.lw, 16)

    rid, pid, off, cols = _send(g, T, topo, core, direct, rank)
    on = topo.mask(core, jobs[0][0]) & ~off
    ids = [DstId(rid=topo.addr(h)[0], pnc=topo.addr(h)[1]) for (h, _) in jobs]
    g.wait_ge(S.ls, 16)
    g.remote_dma_fused([RemoteDMATransfer(dst_ids=ids, dma_engine_mask=on, remote_sem=S.hs,
                                          srcs=[T.wsd[:]], dsts=[T.wsd[:] for _ in jobs])], local_sem=S.sent)
    g.wait_ge(S.lc, 16)
    g.remote_dma_fused([RemoteDMATransfer(dst_ids=ids, dma_engine_mask=on, remote_sem=S.hc,
                                          srcs=[T.wcd[:].bitcast(dt.uint8)],
                                          dsts=[T.wcd[:].bitcast(dt.uint8) for _ in jobs])], local_sem=S.sent)
    g.remote_dma(T.wp[:, cols], T.wsd[:], S["a%d" % rank], S.sent, pid, rid, off)
    g.remote_dma(T.wq[:, cols].bitcast(dt.uint8), T.wcd[:].bitcast(dt.uint8), S["a%d" % rank], S.sent, pid, rid, off)

    place, count = {}, {}
    for j in range(N):
        if j == rank:
            continue
        dj, jj = _routes(T, topo, j)
        if dj == rank:
            place[j], sender = 0, T.cores[j]
        else:
            i = [d for (_, d) in jj].index(rank)
            place[j], sender = 1 + i, jj[i][0]
        count[j] = 2 * _engines(topo.mask(sender, core))
    order = [rank] + sorted(place, key=place.get)

    g.vector.wait_ge(S.lx, 16)
    g.vector.quantize_mx(T.xq[:], T.xp[:], T.xt[:]).then_inc(S.qx, 1)

    g.tensor.wait_ge(S.qx, 1)
    for i, j in enumerate(order):
        blk = slice(NC * j, NC * j + NC)
        wsl = slice(WW * j, WW * j + WW)
        if j == rank:
            g.tensor.wait_ge(S.lw, 32)
        else:
            g.tensor.wait_ge(S["a%d" % j], count[j])
        g.tensor.matmul_mx(T.ps[:, blk], T.wq[:, wsl], T.wp[:, wsl], T.xq[:], T.xp[:], True, True).then_inc(S["m%d" % j], 1)
        if i % 2 == 0:
            g.vector.wait_ge(S["m%d" % j], 1)
            g.vector.tensor_copy(T.yo[:, blk], T.ps[:, blk]).then_inc(S["c%d" % j], 1)
        else:
            g.scalar.wait_ge(S["m%d" % j], 1)
            g.scalar.activation(T.yo[:, blk], T.ps[:, blk], ActivationFunctionType.Copy).then_inc(S["c%d" % j], 1)

    groups = [[j] for j in order]
    if abs(order[4] - order[5]) == 1:
        groups = [[j] for j in order[:4]] + [[order[4], order[5]]] + [[j] for j in order[6:]]
    for grp in groups:
        for j in grp:
            g.sync.wait_ge(S["c%d" % j], 1)
        cols_y = slice(NC * min(grp), NC * max(grp) + NC)
        g.sync.dma_start(T.y[:, cols_y], T.yo[:, cols_y]).then_inc(S.st, 16)
    g.sync.wait_ge(S.st, 16 * len(groups))
    g.wait_ge(S.sent, 2 * _engines(on) + 2 * _engines(off))
